import numpy as np
import ml_dtypes


def mxq(x, axis, fmt="e4m3"):
    dtype, down = {"e4m3": (ml_dtypes.float8_e4m3fn, 7), "e5m2": (ml_dtypes.float8_e5m2, 14)}[fmt]
    v = np.moveaxis(np.asarray(x, np.float32).astype(ml_dtypes.bfloat16).astype(np.float64), axis, -1)
    blocks = v.reshape(v.shape[:-1] + (-1, 32))
    amax = np.abs(blocks).max(-1, keepdims=True)
    byte = np.maximum(np.where(amax > 0, np.frexp(amax)[1] - 1 + 127, 0) - down, 1)
    scale = np.exp2(byte - 127.0)
    codes = (blocks / scale).astype(np.float32).astype(dtype).astype(np.float64)
    return np.moveaxis((codes * scale).reshape(v.shape), -1, axis)


WIDE = False


def mx_kscale(k):
    if not WIDE:
        return np.ones(k)
    levels = np.array([10, -10, 5, -5, 0])
    if k % 512:
        return np.exp2(np.random.permutation(np.resize(levels, k // 32))).repeat(32)
    a = np.empty((k // 512, 16))
    for p in range(k // 512):
        a[p, :8] = np.random.permutation(np.resize(levels, 8))
        for g in range(8):
            far = levels[np.abs(levels - a[p, g]) >= 10]
            a[p, g + 8] = far[np.random.randint(len(far))]
    return np.exp2(a.ravel()).repeat(32)


def f64(x):
    return np.asarray(x).astype(np.float64)


E2M1 = np.array([0.0, 0.5, 1.0, 1.5, 2.0, 3.0, 4.0, 6.0, -0.0, -0.5, -1.0, -1.5, -2.0, -3.0, -4.0, -6.0])


def pack_weight(w, fmt):
    k, n = w.shape
    w = f64(np.asarray(w, np.float32).astype(ml_dtypes.bfloat16)).reshape(k // 32, 32, n)
    amax = np.abs(w).max(1)
    if fmt == "e4m3":
        byte = np.frexp(amax)[1] - 1 + 127 - 7
    else:
        mant, ex = np.frexp(amax / 6.0)
        byte = np.where(mant > 0.5, ex, ex - 1) + 127
    byte = np.clip(np.where(amax > 0, byte, 1), 1, 254)
    scaled = (w * np.exp2(127.0 - byte)[:, None, :]).reshape(k, n).astype(np.float32)
    by_word = np.ascontiguousarray(scaled.reshape(k // 512, 128, 4, n).transpose(0, 1, 3, 2))
    if fmt == "e4m3":
        words = by_word.astype(ml_dtypes.float8_e4m3fn).view(np.uint8)
    else:
        c = by_word.astype(ml_dtypes.float4_e2m1fn).view(np.uint8) & 0xF
        words = (c[..., 0::2] | (c[..., 1::2] << 4)).reshape(k // 512, 128, 2 * n)
    return np.ascontiguousarray(words), np.ascontiguousarray(byte.astype(np.uint8).reshape(k // 512, 16, n))


def unpack_weight(words, scales, fmt):
    g, _, n = scales.shape
    words = np.ascontiguousarray(words).reshape(g, 128, n, -1)
    if fmt == "e4m3":
        vals = words.view(ml_dtypes.float8_e4m3fn).astype(np.float64)
    else:
        nib = np.empty((g, 128, n, 4), np.uint8)
        nib[..., 0::2] = words & 0xF
        nib[..., 1::2] = words >> 4
        vals = E2M1[nib]
    vals = vals * np.repeat(np.exp2(scales.astype(np.float64) - 127.0), 8, axis=1)[..., None]
    return vals.transpose(0, 1, 3, 2).reshape(g * 512, n)


K, M, T = 2048, 512, 1024


def setup_inputs():
    n = np.random.standard_normal
    s = mx_kscale(K)[:, None]
    w = n((K, M)) / np.sqrt(K) / s
    w4 = pack_weight(w, "e2m1")
    rest = w - unpack_weight(*w4, "e2m1")
    p_r8 = pack_weight(rest, "e4m3")
    return {
        "x": (n((K, T)) * s).astype(np.float32),
        "w4_words": w4[0],
        "w4_scales": w4[1],
        "r8_words": p_r8[0],
        "r8_scales": p_r8[1],
        "g": (n((512, 1024))).astype(np.float32),
    }


def reference(x, w4_words, w4_scales, r8_words, r8_scales, g):
    x_ = mxq(f64(x), 0, "e4m3")
    w4_ = unpack_weight(w4_words, w4_scales, "e2m1")
    r8_ = unpack_weight(r8_words, r8_scales, "e4m3")
    y = w4_.T @ x_ + r8_.T @ x_
    return f64(g) * y

@@ -1,0 +1,166 @@
+from contextlib import ExitStack
+
+import concourse.mybir as mybir
+
+K, N, T = 2048, 512, 1024
+
+F32 = mybir.dt.float32
+BF16 = mybir.dt.bfloat16
+I32 = mybir.dt.int32
+U32 = mybir.dt.uint32
+U8 = mybir.dt.uint8
+FP8X4 = mybir.dt.float8_e4m3fn_x4
+FP4X4 = mybir.dt.float4_e2m1fn_x4
+
+FLOPS = 2 * 2 * K * N * T
+
+P = 128
+PACK = 4
+K_PASS = P * PACK
+PASSES = K // K_PASS
+M_TILES = N // P
+T_TILE = 512
+HALVES = T // T_TILE
+QUADS = 4
+
+ORDER = ((0, 0), (1, 0), (0, 1), (1, 1), (2, 0), (2, 1), (3, 0), (3, 1))
+CHUNK = 256
+V_COLS = 168
+V_COLS_LAST = 144
+
+
+def tile_mix_resid_fm_mul_kernel(tc, x, w4_words, w4_scales, r8_words, r8_scales, g, out):
+    nc = tc.nc
+    with ExitStack() as ctx:
+        keep = ctx.enter_context(tc.tile_pool(name="keep", bufs=1))
+        psum = ctx.enter_context(tc.psum_pool(name="psum", bufs=1))
+
+        r8_plane = keep.tile([P, N], U8, name="r8_plane", align_bytes=64)
+        w4_plane = keep.tile([P, PASSES, N], U8, name="w4_plane", align_bytes=64)
+        warm = keep.tile([P, 8], F32, name="warm")
+        x_raw = []
+        r8_codes = []
+        w4_codes = []
+        for a in range(PASSES):
+            x_raw.append(keep.tile([P, PACK, T], F32, name="x_raw%d" % a, align_bytes=64))
+            r8_codes.append(keep.tile([P, 4 * N], U8, name="r8_codes%d" % a, align_bytes=64))
+            w4_codes.append(keep.tile([P, 2 * N], U8, name="w4_codes%d" % a, align_bytes=64))
+        grouped = {}
+        codes = {}
+        scales = {}
+        for a in range(PASSES):
+            for h in range(HALVES):
+                grouped[a, h] = keep.tile([P, T_TILE, PACK], BF16, name="grouped%d%d" % (a, h), align_bytes=64)
+                codes[a, h] = keep.tile([P, T_TILE], U32, name="codes%d%d" % (a, h), align_bytes=64)
+                scales[a, h] = keep.tile([P, T_TILE], U8, name="scales%d%d" % (a, h), align_bytes=64)
+        g_sb = []
+        o_sb = []
+        acc = {}
+        for m in range(M_TILES):
+            g_sb.append(keep.tile([P, T], F32, name="g%d" % m))
+            o_sb.append(keep.tile([P, T], F32, name="o%d" % m))
+            for h in range(HALVES):
+                acc[m, h] = psum.tile([P, T_TILE], F32, name="acc%d%d" % (m, h))
+
+        def load_x(a):
+            nc.sync.dma_start(
+                out=x_raw[a][:], in_=x[a * K_PASS : (a + 1) * K_PASS, :].rearrange("(p j) t -> p j t", j=PACK)
+            )
+
+        def load_w(a):
+            nc.sync.dma_start(
+                out=r8_codes[a][:].bitcast(I32), in_=r8_words[a].rearrange("p n i -> p (n i)").bitcast(I32)
+            )
+            nc.sync.dma_start(out=w4_codes[a][:].bitcast(I32), in_=w4_words[a].bitcast(I32))
+
+        def interleave(copy, a, h, lo, hi):
+            copy(
+                out=grouped[a, h][:, lo:hi, :].rearrange("p (c i) j -> p c j i", i=4),
+                in_=x_raw[a][:, :, h * T_TILE + lo : h * T_TILE + hi].rearrange("p j (c i) -> p c j i", i=4),
+            )
+
+        def quantize(a, h, lo, hi):
+            nc.vector.quantize_mx(
+                out=codes[a, h][:, lo:hi].bitcast(FP8X4),
+                scales=scales[a, h][:, lo:hi],
+                in_=grouped[a, h][:, lo:hi, :].rearrange("p c j -> p (c j)"),
+            )
+
+        def prepare(a):
+            for h in range(HALVES):
+                v_cols = V_COLS_LAST if (a, h) == (PASSES - 1, 1) else V_COLS
+                for lo in range(0, T_TILE, CHUNK):
+                    interleave(nc.scalar.copy, a, h, lo + v_cols, lo + CHUNK)
+                for lo in range(0, T_TILE, CHUNK):
+                    interleave(nc.vector.tensor_copy, a, h, lo, lo + v_cols)
+                for lo in range(0, T_TILE, CHUNK):
+                    quantize(a, h, lo, lo + CHUNK)
+
+        def multiply_r8(a, m, h):
+            nc.tensor.matmul_mx(
+                out=acc[m, h][:],
+                lhsT=r8_codes[a][:, 4 * P * m : 4 * P * (m + 1)].bitcast(FP8X4),
+                lhsT_scale=r8_plane[4 * a : P, P * m : P * (m + 1)],
+                rhs=codes[a, h][:].bitcast(FP8X4),
+                rhs_scale=scales[a, h][:],
+                start=(a == 0),
+                stop=False,
+            )
+
+        def multiply_w4(a, m, h):
+            nc.tensor.matmul_mx(
+                out=acc[m, h][:],
+                lhsT=w4_codes[a][:, 2 * P * m : 2 * P * (m + 1)].bitcast(FP4X4),
+                lhsT_scale=w4_plane[:, a, P * m : P * (m + 1)],
+                rhs=codes[a, h][:].bitcast(FP8X4),
+                rhs_scale=scales[a, h][:],
+                start=False,
+                stop=(a == PASSES - 1),
+            )
+
+        with tc.manual_schedule():
+            nc.vector.memset(warm[:], 0.0)
+            nc.scalar.copy(out=warm[:, 0:1], in_=warm[:, 4:5])
+            nc.vector.memset(r8_plane[:].bitcast(I32), 0)
+            nc.vector.memset(w4_plane[:].rearrange("p a n -> p (a n)").bitcast(I32), 0)
+
+            load_x(0)
+            for q in range(QUADS):
+                nc.sync.dma_start(
+                    out=r8_plane[:].bitcast(I32)[32 * q : 32 * q + 16, :],
+                    in_=r8_scales[:, 4 * q : 4 * q + 4, :].bitcast(I32),
+                )
+            load_w(0)
+            load_x(1)
+            for q in range(QUADS):
+                nc.sync.dma_start(
+                    out=w4_plane[32 * q : 32 * q + 4, :, :].bitcast(I32),
+                    in_=w4_scales[:, 4 * q : 4 * q + 4, :].rearrange("a r n -> r a n").bitcast(I32),
+                )
+            load_w(1)
+            for a in range(2, PASSES):
+                load_x(a)
+                load_w(a)
+            for m in range(M_TILES):
+                nc.sync.dma_start(out=g_sb[m][:], in_=g[m * P : (m + 1) * P, :])
+
+            for a in range(PASSES - 1):
+                prepare(a)
+                for h in range(HALVES):
+                    for m in range(M_TILES):
+                        multiply_r8(a, m, h)
+                for h in range(HALVES):
+                    for m in range(M_TILES):
+                        multiply_w4(a, m, h)
+
+            prepare(PASSES - 1)
+            for m, h in ORDER:
+                multiply_r8(PASSES - 1, m, h)
+                multiply_w4(PASSES - 1, m, h)
+            for m, h in ORDER:
+                cols = slice(h * T_TILE, (h + 1) * T_TILE)
+                nc.vector.tensor_tensor(
+                    out=o_sb[m][:, cols], in0=acc[m, h][:], in1=g_sb[m][:, cols], op=mybir.AluOpType.mult
+                )
+                queue = nc.sync if h == 0 else nc.scalar
+                queue.dma_start(out=out[m * P : (m + 1) * P, cols], in_=o_sb[m][:, cols])

@@ -132,10 +132,10 @@ def tile_mix_resid_fm_mul_kernel(tc, x, w4_words, w4_scales, r8_words, r8_scales
                 )
             load_w(0)
             load_x(1)
-            for q in range(QUADS):
+            for r in range(4):
                 nc.sync.dma_start(
-                    out=w4_plane[32 * q : 32 * q + 4, :, :].bitcast(I32),
-                    in_=w4_scales[:, 4 * q : 4 * q + 4, :].rearrange("a r n -> r a n").bitcast(I32),
+                    out=w4_plane[r:P:32, :, :].bitcast(I32),
+                    in_=w4_scales[:, r:16:4, :].rearrange("a q n -> q a n").bitcast(I32),
                 )
             load_w(1)
             for a in range(2, PASSES):

@@ -24,6 +24,8 @@ HALVES = T // T_TILE
 QUADS = 4
 
 ORDER = ((0, 0), (1, 0), (0, 1), (1, 1), (2, 0), (2, 1), (3, 0), (3, 1))
+W_LOADS = ((0, 1), (1, 3), (3, 4))
+G_LOADS = ((0, 1), (1, 2), (2, 3), (3, 4))
 CHUNK = 256
 V_COLS = 168
 V_COLS_LAST = 144
@@ -37,14 +39,19 @@ def tile_mix_resid_fm_mul_kernel(tc, x, w4_words, w4_scales, r8_words, r8_scales
 
         r8_plane = keep.tile([P, N], U8, name="r8_plane", align_bytes=64)
         w4_plane = keep.tile([P, PASSES, N], U8, name="w4_plane", align_bytes=64)
-        warm = keep.tile([P, 8], F32, name="warm")
         x_raw = []
+        r8_tiles = []
+        w4_tiles = []
         r8_codes = []
         w4_codes = []
+        for lo, hi in W_LOADS:
+            r8_tiles.append(keep.tile([P, hi - lo, 4 * N], U8, name="r8_codes%d" % lo, align_bytes=64))
+            w4_tiles.append(keep.tile([P, hi - lo, 2 * N], U8, name="w4_codes%d" % lo, align_bytes=64))
+            for a in range(lo, hi):
+                r8_codes.append(r8_tiles[-1][:, a - lo, :])
+                w4_codes.append(w4_tiles[-1][:, a - lo, :])
         for a in range(PASSES):
             x_raw.append(keep.tile([P, PACK, T], F32, name="x_raw%d" % a, align_bytes=64))
-            r8_codes.append(keep.tile([P, 4 * N], U8, name="r8_codes%d" % a, align_bytes=64))
-            w4_codes.append(keep.tile([P, 2 * N], U8, name="w4_codes%d" % a, align_bytes=64))
         grouped = {}
         codes = {}
         scales = {}
@@ -53,11 +60,15 @@ def tile_mix_resid_fm_mul_kernel(tc, x, w4_words, w4_scales, r8_words, r8_scales
                 grouped[a, h] = keep.tile([P, T_TILE, PACK], BF16, name="grouped%d%d" % (a, h), align_bytes=64)
                 codes[a, h] = keep.tile([P, T_TILE], U32, name="codes%d%d" % (a, h), align_bytes=64)
                 scales[a, h] = keep.tile([P, T_TILE], U8, name="scales%d%d" % (a, h), align_bytes=64)
+        g_pairs = []
         g_sb = []
+        for lo, hi in G_LOADS:
+            g_pairs.append(keep.tile([P, hi - lo, T], F32, name="g%d" % lo))
+            for m in range(lo, hi):
+                g_sb.append(g_pairs[-1][:, m - lo, :])
         o_sb = []
         acc = {}
         for m in range(M_TILES):
-            g_sb.append(keep.tile([P, T], F32, name="g%d" % m))
             o_sb.append(keep.tile([P, T], F32, name="o%d" % m))
             for h in range(HALVES):
                 acc[m, h] = psum.tile([P, T_TILE], F32, name="acc%d%d" % (m, h))
@@ -67,11 +78,14 @@ def tile_mix_resid_fm_mul_kernel(tc, x, w4_words, w4_scales, r8_words, r8_scales
                 out=x_raw[a][:], in_=x[a * K_PASS : (a + 1) * K_PASS, :].rearrange("(p j) t -> p j t", j=PACK)
             )
 
-        def load_w(a):
+        def load_w(i):
+            lo, hi = W_LOADS[i]
             nc.sync.dma_start(
-                out=r8_codes[a][:].bitcast(I32), in_=r8_words[a].rearrange("p n i -> p (n i)").bitcast(I32)
+                out=r8_tiles[i][:].bitcast(I32), in_=r8_words[lo:hi].rearrange("a p n i -> p a (n i)").bitcast(I32)
             )
-            nc.sync.dma_start(out=w4_codes[a][:].bitcast(I32), in_=w4_words[a].bitcast(I32))
+            nc.sync.dma_start(
+                out=w4_tiles[i][:].bitcast(I32), in_=w4_words[lo:hi].rearrange("a p n -> p a n").bitcast(I32)
+            )
 
         def interleave(copy, a, h, lo, hi):
             copy(
@@ -119,8 +133,6 @@ def tile_mix_resid_fm_mul_kernel(tc, x, w4_words, w4_scales, r8_words, r8_scales
             )
 
         with tc.manual_schedule():
-            nc.vector.memset(warm[:], 0.0)
-            nc.scalar.copy(out=warm[:, 0:1], in_=warm[:, 4:5])
             nc.vector.memset(r8_plane[:].bitcast(I32), 0)
             nc.vector.memset(w4_plane[:].rearrange("p a n -> p (a n)").bitcast(I32), 0)
 
@@ -138,11 +150,12 @@ def tile_mix_resid_fm_mul_kernel(tc, x, w4_words, w4_scales, r8_words, r8_scales
                     in_=w4_scales[:, r:16:4, :].rearrange("a q n -> q a n").bitcast(I32),
                 )
             load_w(1)
-            for a in range(2, PASSES):
-                load_x(a)
-                load_w(a)
-            for m in range(M_TILES):
-                nc.sync.dma_start(out=g_sb[m][:], in_=g[m * P : (m + 1) * P, :])
+            load_x(2)
+            load_x(3)
+            load_w(2)
+            for i, (lo, hi) in enumerate(G_LOADS):
+                rows = g[lo * P : hi * P, :]
+                nc.sync.dma_start(out=g_pairs[i][:], in_=rows.rearrange("(m p) t -> p m t", p=P))
 
             for a in range(PASSES - 1):
                 prepare(a)

@@ -35,6 +35,7 @@ def tile_mix_resid_fm_mul_kernel(tc, x, w4_words, w4_scales, r8_words, r8_scales
     nc = tc.nc
     with ExitStack() as ctx:
         keep = ctx.enter_context(tc.tile_pool(name="keep", bufs=1))
+        rows_pool = ctx.enter_context(tc.tile_pool(name="rows", bufs=1))
         psum = ctx.enter_context(tc.psum_pool(name="psum", bufs=1))
 
         r8_plane = keep.tile([P, N], U8, name="r8_plane", align_bytes=64)
@@ -51,7 +52,7 @@ def tile_mix_resid_fm_mul_kernel(tc, x, w4_words, w4_scales, r8_words, r8_scales
                 r8_codes.append(r8_tiles[-1][:, a - lo, :])
                 w4_codes.append(w4_tiles[-1][:, a - lo, :])
         for a in range(PASSES):
-            x_raw.append(keep.tile([P, PACK, T], F32, name="x_raw%d" % a, align_bytes=64))
+            x_raw.append(rows_pool.tile([P, PACK, T], F32, name="x_raw%d" % a, align_bytes=256))
         grouped = {}
         codes = {}
         scales = {}
@@ -63,13 +64,13 @@ def tile_mix_resid_fm_mul_kernel(tc, x, w4_words, w4_scales, r8_words, r8_scales
         g_pairs = []
         g_sb = []
         for lo, hi in G_LOADS:
-            g_pairs.append(keep.tile([P, hi - lo, T], F32, name="g%d" % lo))
+            g_pairs.append(rows_pool.tile([P, hi - lo, T], F32, name="g%d" % lo, align_bytes=256))
             for m in range(lo, hi):
                 g_sb.append(g_pairs[-1][:, m - lo, :])
         o_sb = []
         acc = {}
         for m in range(M_TILES):
-            o_sb.append(keep.tile([P, T], F32, name="o%d" % m))
+            o_sb.append(rows_pool.tile([P, T], F32, name="o%d" % m, align_bytes=256))
             for h in range(HALVES):
                 acc[m, h] = psum.tile([P, T_TILE], F32, name="acc%d%d" % (m, h))
 

@@ -28,7 +28,7 @@ W_LOADS = ((0, 1), (1, 3), (3, 4))
 G_LOADS = ((0, 1), (1, 2), (2, 3), (3, 4))
 CHUNK = 256
 V_COLS = 168
-V_COLS_LAST = 144
+V_COLS_LAST = 104
 
 
 def tile_mix_resid_fm_mul_kernel(tc, x, w4_words, w4_scales, r8_words, r8_scales, g, out):
@@ -160,12 +160,13 @@ def tile_mix_resid_fm_mul_kernel(tc, x, w4_words, w4_scales, r8_words, r8_scales
 
             for a in range(PASSES - 1):
                 prepare(a)
-                for h in range(HALVES):
+                if a == 0:
+                    steps = [(multiply, h) for multiply in (multiply_r8, multiply_w4) for h in range(HALVES)]
+                else:
+                    steps = [(multiply, h) for h in range(HALVES) for multiply in (multiply_r8, multiply_w4)]
+                for multiply, h in steps:
                     for m in range(M_TILES):
-                        multiply_r8(a, m, h)
-                for h in range(HALVES):
-                    for m in range(M_TILES):
-                        multiply_w4(a, m, h)
+                        multiply(a, m, h)
 
             prepare(PASSES - 1)
             for m, h in ORDER:

@@ -161,7 +161,7 @@ def tile_mix_resid_fm_mul_kernel(tc, x, w4_words, w4_scales, r8_words, r8_scales
             for a in range(PASSES - 1):
                 prepare(a)
                 if a == 0:
-                    steps = [(multiply, h) for multiply in (multiply_r8, multiply_w4) for h in range(HALVES)]
+                    steps = [(multiply, h) for multiply in (multiply_r8, multiply_w4) for h in reversed(range(HALVES))]
                 else:
                     steps = [(multiply, h) for h in range(HALVES) for multiply in (multiply_r8, multiply_w4)]
                 for multiply, h in steps:

@@ -18,14 +18,15 @@ P = 128
 PACK = 4
 K_PASS = P * PACK
 PASSES = K // K_PASS
+LAST = PASSES - 1
 M_TILES = N // P
 T_TILE = 512
 HALVES = T // T_TILE
 QUADS = 4
 
+R8_LOADS = ((0, 1), (1, 2), (2, 3), (3, 4))
+W4_LOADS = ((0, 1), (1, 2), (2, 3), (3, 4))
 ORDER = ((0, 0), (1, 0), (0, 1), (1, 1), (2, 0), (2, 1), (3, 0), (3, 1))
-W_LOADS = ((0, 1), (1, 3), (3, 4))
-G_LOADS = ((0, 1), (1, 2), (2, 3), (3, 4))
 CHUNK = 256
 V_COLS = 168
 V_COLS_LAST = 104
@@ -40,17 +41,19 @@ def tile_mix_resid_fm_mul_kernel(tc, x, w4_words, w4_scales, r8_words, r8_scales
 
         r8_plane = keep.tile([P, N], U8, name="r8_plane", align_bytes=64)
         w4_plane = keep.tile([P, PASSES, N], U8, name="w4_plane", align_bytes=64)
-        x_raw = []
         r8_tiles = []
         w4_tiles = []
         r8_codes = []
         w4_codes = []
-        for lo, hi in W_LOADS:
+        for lo, hi in R8_LOADS:
             r8_tiles.append(keep.tile([P, hi - lo, 4 * N], U8, name="r8_codes%d" % lo, align_bytes=64))
-            w4_tiles.append(keep.tile([P, hi - lo, 2 * N], U8, name="w4_codes%d" % lo, align_bytes=64))
             for a in range(lo, hi):
                 r8_codes.append(r8_tiles[-1][:, a - lo, :])
+        for lo, hi in W4_LOADS:
+            w4_tiles.append(keep.tile([P, hi - lo, 2 * N], U8, name="w4_codes%d" % lo, align_bytes=64))
+            for a in range(lo, hi):
                 w4_codes.append(w4_tiles[-1][:, a - lo, :])
+        x_raw = []
         for a in range(PASSES):
             x_raw.append(rows_pool.tile([P, PACK, T], F32, name="x_raw%d" % a, align_bytes=256))
         grouped = {}
@@ -61,117 +64,129 @@ def tile_mix_resid_fm_mul_kernel(tc, x, w4_words, w4_scales, r8_words, r8_scales
                 grouped[a, h] = keep.tile([P, T_TILE, PACK], BF16, name="grouped%d%d" % (a, h), align_bytes=64)
                 codes[a, h] = keep.tile([P, T_TILE], U32, name="codes%d%d" % (a, h), align_bytes=64)
                 scales[a, h] = keep.tile([P, T_TILE], U8, name="scales%d%d" % (a, h), align_bytes=64)
-        g_pairs = []
         g_sb = []
-        for lo, hi in G_LOADS:
-            g_pairs.append(rows_pool.tile([P, hi - lo, T], F32, name="g%d" % lo, align_bytes=256))
-            for m in range(lo, hi):
-                g_sb.append(g_pairs[-1][:, m - lo, :])
         o_sb = []
         acc = {}
+        for m in range(M_TILES):
+            g_sb.append(rows_pool.tile([P, T], F32, name="g%d" % m, align_bytes=256))
         for m in range(M_TILES):
             o_sb.append(rows_pool.tile([P, T], F32, name="o%d" % m, align_bytes=256))
             for h in range(HALVES):
                 acc[m, h] = psum.tile([P, T_TILE], F32, name="acc%d%d" % (m, h))
 
         def load_x(a):
-            nc.sync.dma_start(
-                out=x_raw[a][:], in_=x[a * K_PASS : (a + 1) * K_PASS, :].rearrange("(p j) t -> p j t", j=PACK)
-            )
+            rows = x[a * K_PASS : (a + 1) * K_PASS, :]
+            nc.sync.dma_start(out=x_raw[a][:], in_=rows.rearrange("(p j) t -> p j t", j=PACK))
 
-        def load_w(i):
-            lo, hi = W_LOADS[i]
+        def load_r8(i):
+            lo, hi = R8_LOADS[i]
             nc.sync.dma_start(
                 out=r8_tiles[i][:].bitcast(I32), in_=r8_words[lo:hi].rearrange("a p n i -> p a (n i)").bitcast(I32)
             )
+
+        def load_w4(i):
+            lo, hi = W4_LOADS[i]
             nc.sync.dma_start(
                 out=w4_tiles[i][:].bitcast(I32), in_=w4_words[lo:hi].rearrange("a p n -> p a n").bitcast(I32)
             )
 
-        def interleave(copy, a, h, lo, hi):
+        def load_r8_scales(quads):
+            for q in quads:
+                nc.sync.dma_start(
+                    out=r8_plane[:].bitcast(I32)[32 * q : 32 * q + 16, :],
+                    in_=r8_scales[:, 4 * q : 4 * q + 4, :].bitcast(I32),
+                )
+
+        def load_w4_scales():
+            for r in range(4):
+                nc.sync.dma_start(
+                    out=w4_plane[r:P:32, :, :].bitcast(I32),
+                    in_=w4_scales[:, r:16:4, :].rearrange("a q n -> q a n").bitcast(I32),
+                )
+
+        def interleave(copy, a, lo, hi):
+            h, col = divmod(lo, T_TILE)
             copy(
-                out=grouped[a, h][:, lo:hi, :].rearrange("p (c i) j -> p c j i", i=4),
-                in_=x_raw[a][:, :, h * T_TILE + lo : h * T_TILE + hi].rearrange("p j (c i) -> p c j i", i=4),
+                out=grouped[a, h][:, col : col + hi - lo, :].rearrange("p (c i) j -> p c j i", i=4),
+                in_=x_raw[a][:, :, lo:hi].rearrange("p j (c i) -> p c j i", i=4),
             )
 
-        def quantize(a, h, lo, hi):
+        def quantize(a, lo, hi):
+            h, col = divmod(lo, T_TILE)
             nc.vector.quantize_mx(
-                out=codes[a, h][:, lo:hi].bitcast(FP8X4),
-                scales=scales[a, h][:, lo:hi],
-                in_=grouped[a, h][:, lo:hi, :].rearrange("p c j -> p (c j)"),
+                out=codes[a, h][:, col : col + hi - lo].bitcast(FP8X4),
+                scales=scales[a, h][:, col : col + hi - lo],
+                in_=grouped[a, h][:, col : col + hi - lo, :].rearrange("p c j -> p (c j)"),
             )
 
-        def prepare(a):
-            for h in range(HALVES):
-                v_cols = V_COLS_LAST if (a, h) == (PASSES - 1, 1) else V_COLS
-                for lo in range(0, T_TILE, CHUNK):
-                    interleave(nc.scalar.copy, a, h, lo + v_cols, lo + CHUNK)
-                for lo in range(0, T_TILE, CHUNK):
-                    interleave(nc.vector.tensor_copy, a, h, lo, lo + v_cols)
-                for lo in range(0, T_TILE, CHUNK):
-                    quantize(a, h, lo, lo + CHUNK)
+        def prepare(a, first, end):
+            v_cols = V_COLS_LAST if (a, first) == (LAST, T_TILE) else V_COLS
+            chunks = range(first, end, CHUNK)
+            for lo in chunks:
+                interleave(nc.scalar.copy, a, lo + v_cols, lo + CHUNK)
+            for lo in chunks:
+                interleave(nc.vector.tensor_copy, a, lo, lo + v_cols)
+            for lo in chunks:
+                quantize(a, lo, lo + CHUNK)
 
-        def multiply_r8(a, m, h):
+        def multiply_r8(a, m, h, lo=0, hi=T_TILE):
             nc.tensor.matmul_mx(
-                out=acc[m, h][:],
+                out=acc[m, h][:, lo:hi],
                 lhsT=r8_codes[a][:, 4 * P * m : 4 * P * (m + 1)].bitcast(FP8X4),
                 lhsT_scale=r8_plane[4 * a : P, P * m : P * (m + 1)],
-                rhs=codes[a, h][:].bitcast(FP8X4),
-                rhs_scale=scales[a, h][:],
-                start=(a == 0),
+                rhs=codes[a, h][:, lo:hi].bitcast(FP8X4),
+                rhs_scale=scales[a, h][:, lo:hi],
+                start=(a == 0 and lo == 0),
                 stop=False,
             )
 
-        def multiply_w4(a, m, h):
+        def multiply_w4(a, m, h, lo=0, hi=T_TILE):
             nc.tensor.matmul_mx(
-                out=acc[m, h][:],
+                out=acc[m, h][:, lo:hi],
                 lhsT=w4_codes[a][:, 2 * P * m : 2 * P * (m + 1)].bitcast(FP4X4),
                 lhsT_scale=w4_plane[:, a, P * m : P * (m + 1)],
-                rhs=codes[a, h][:].bitcast(FP8X4),
-                rhs_scale=scales[a, h][:],
+                rhs=codes[a, h][:, lo:hi].bitcast(FP8X4),
+                rhs_scale=scales[a, h][:, lo:hi],
                 start=False,
-                stop=(a == PASSES - 1),
+                stop=(a == LAST),
             )
+
+        steps = [[(multiply, 0, h, 0, T_TILE) for multiply in (multiply_r8, multiply_w4) for h in range(HALVES)]]
+        for a in range(1, LAST):
+            steps.append([(multiply, a, h, 0, T_TILE) for h in range(HALVES) for multiply in (multiply_r8, multiply_w4)])
 
         with tc.manual_schedule():
             nc.vector.memset(r8_plane[:].bitcast(I32), 0)
             nc.vector.memset(w4_plane[:].rearrange("p a n -> p (a n)").bitcast(I32), 0)
 
             load_x(0)
-            for q in range(QUADS):
-                nc.sync.dma_start(
-                    out=r8_plane[:].bitcast(I32)[32 * q : 32 * q + 16, :],
-                    in_=r8_scales[:, 4 * q : 4 * q + 4, :].bitcast(I32),
-                )
-            load_w(0)
+            load_r8_scales(range(QUADS))
+            load_r8(0)
+            load_w4(0)
             load_x(1)
-            for r in range(4):
-                nc.sync.dma_start(
-                    out=w4_plane[r:P:32, :, :].bitcast(I32),
-                    in_=w4_scales[:, r:16:4, :].rearrange("a q n -> q a n").bitcast(I32),
-                )
-            load_w(1)
-            load_x(2)
-            load_x(3)
-            load_w(2)
-            for i, (lo, hi) in enumerate(G_LOADS):
-                rows = g[lo * P : hi * P, :]
-                nc.sync.dma_start(out=g_pairs[i][:], in_=rows.rearrange("(m p) t -> p m t", p=P))
+            load_w4_scales()
+            load_r8(1)
+            load_w4(1)
+            for a in range(2, PASSES):
+                load_x(a)
+                load_r8(a)
+                load_w4(a)
+            for m in range(M_TILES):
+                nc.sync.dma_start(out=g_sb[m][:], in_=g[m * P : (m + 1) * P, :])
 
-            for a in range(PASSES - 1):
-                prepare(a)
-                if a == 0:
-                    steps = [(multiply, h) for multiply in (multiply_r8, multiply_w4) for h in reversed(range(HALVES))]
-                else:
-                    steps = [(multiply, h) for h in range(HALVES) for multiply in (multiply_r8, multiply_w4)]
-                for multiply, h in steps:
+            for a in range(LAST):
+                width = T if a == 0 else T_TILE
+                for first in range(0, T, width):
+                    prepare(a, first, first + width)
+                for multiply, b, h, lo, hi in steps[a]:
                     for m in range(M_TILES):
-                        multiply(a, m, h)
+                        multiply(b, m, h, lo, hi)
 
-            prepare(PASSES - 1)
+            for first in range(0, T, T_TILE):
+                prepare(LAST, first, first + T_TILE)
             for m, h in ORDER:
-                multiply_r8(PASSES - 1, m, h)
-                multiply_w4(PASSES - 1, m, h)
+                multiply_r8(LAST, m, h)
+                multiply_w4(LAST, m, h)
             for m, h in ORDER:
                 cols = slice(h * T_TILE, (h + 1) * T_TILE)
                 nc.vector.tensor_tensor(

@@ -26,7 +26,6 @@ QUADS = 4
 
 R8_LOADS = ((0, 1), (1, 2), (2, 3), (3, 4))
 W4_LOADS = ((0, 1), (1, 2), (2, 3), (3, 4))
-ORDER = ((0, 0), (1, 0), (0, 1), (1, 1), (2, 0), (2, 1), (3, 0), (3, 1))
 CHUNK = 256
 V_COLS = 168
 V_COLS_LAST = 104
@@ -67,6 +66,7 @@ def tile_mix_resid_fm_mul_kernel(tc, x, w4_words, w4_scales, r8_words, r8_scales
         g_sb = []
         o_sb = []
         acc = {}
+        drained = rows_pool.tile([P, T_TILE], F32, name="drained", align_bytes=256)
         for m in range(M_TILES):
             g_sb.append(rows_pool.tile([P, T], F32, name="g%d" % m, align_bytes=256))
         for m in range(M_TILES):
@@ -148,7 +148,7 @@ def tile_mix_resid_fm_mul_kernel(tc, x, w4_words, w4_scales, r8_words, r8_scales
                 rhs=codes[a, h][:, lo:hi].bitcast(FP8X4),
                 rhs_scale=scales[a, h][:, lo:hi],
                 start=False,
-                stop=(a == LAST),
+                stop=(a == LAST and hi == T_TILE),
             )
 
         steps = [[(multiply, 0, h, 0, T_TILE) for multiply in (multiply_r8, multiply_w4) for h in range(HALVES)]]
@@ -184,13 +184,23 @@ def tile_mix_resid_fm_mul_kernel(tc, x, w4_words, w4_scales, r8_words, r8_scales
 
             for first in range(0, T, T_TILE):
                 prepare(LAST, first, first + T_TILE)
-            for m, h in ORDER:
+            for lo in range(0, T_TILE, CHUNK):
+                for m in range(2):
+                    multiply_r8(LAST, m, 0, lo, lo + CHUNK)
+                    multiply_w4(LAST, m, 0, lo, lo + CHUNK)
+            for m, h in ((2, 0), (0, 1), (1, 1), (2, 1), (3, 0), (3, 1)):
                 multiply_r8(LAST, m, h)
                 multiply_w4(LAST, m, h)
-            for m, h in ORDER:
+            nc.scalar.copy(out=drained[:], in_=acc[2, 0][:])
+            nc.gpsimd.tensor_tensor(
+                out=o_sb[2][:, :T_TILE], in0=drained[:], in1=g_sb[2][:, :T_TILE], op=mybir.AluOpType.mult
+            )
+            for m, h in ((0, 0), (1, 0), (0, 1), (1, 1), (2, 1), (3, 0), (3, 1)):
                 cols = slice(h * T_TILE, (h + 1) * T_TILE)
                 nc.vector.tensor_tensor(
                     out=o_sb[m][:, cols], in0=acc[m, h][:], in1=g_sb[m][:, cols], op=mybir.AluOpType.mult
                 )
-                queue = nc.sync if h == 0 else nc.scalar
-                queue.dma_start(out=out[m * P : (m + 1) * P, cols], in_=o_sb[m][:, cols])
+                if m < 2:
+                    nc.sync.dma_start(out=out[m * P : (m + 1) * P, cols], in_=o_sb[m][:, cols])
+                elif h == 1:
+                    nc.sync.dma_start(out=out[m * P : (m + 1) * P, :], in_=o_sb[m][:])

@@ -200,7 +200,6 @@ def tile_mix_resid_fm_mul_kernel(tc, x, w4_words, w4_scales, r8_words, r8_scales
                 nc.vector.tensor_tensor(
                     out=o_sb[m][:, cols], in0=acc[m, h][:], in1=g_sb[m][:, cols], op=mybir.AluOpType.mult
                 )
-                if m < 2:
-                    nc.sync.dma_start(out=out[m * P : (m + 1) * P, cols], in_=o_sb[m][:, cols])
-                elif h == 1:
-                    nc.sync.dma_start(out=out[m * P : (m + 1) * P, :], in_=o_sb[m][:])
+                nc.sync.dma_start(out=out[m * P : (m + 1) * P, cols], in_=o_sb[m][:, cols])
+                if (m, h) == (2, 1):
+                    nc.sync.dma_start(out=out[m * P : (m + 1) * P, :T_TILE], in_=o_sb[m][:, :T_TILE])

@@ -11,6 +11,7 @@ U32 = mybir.dt.uint32
 U8 = mybir.dt.uint8
 FP8X4 = mybir.dt.float8_e4m3fn_x4
 FP4X4 = mybir.dt.float4_e2m1fn_x4
+MULT = mybir.AluOpType.mult
 
 FLOPS = 2 * 2 * K * N * T
 
@@ -23,12 +24,10 @@ M_TILES = N // P
 T_TILE = 512
 HALVES = T // T_TILE
 QUADS = 4
-
-R8_LOADS = ((0, 1), (1, 2), (2, 3), (3, 4))
-W4_LOADS = ((0, 1), (1, 2), (2, 3), (3, 4))
 CHUNK = 256
 V_COLS = 168
-V_COLS_LAST = 104
+V_COLS_LATE = (144, 96)
+V_COLS_EARLY = 336
 
 
 def tile_mix_resid_fm_mul_kernel(tc, x, w4_words, w4_scales, r8_words, r8_scales, g, out):
@@ -40,21 +39,9 @@ def tile_mix_resid_fm_mul_kernel(tc, x, w4_words, w4_scales, r8_words, r8_scales
 
         r8_plane = keep.tile([P, N], U8, name="r8_plane", align_bytes=64)
         w4_plane = keep.tile([P, PASSES, N], U8, name="w4_plane", align_bytes=64)
-        r8_tiles = []
-        w4_tiles = []
-        r8_codes = []
-        w4_codes = []
-        for lo, hi in R8_LOADS:
-            r8_tiles.append(keep.tile([P, hi - lo, 4 * N], U8, name="r8_codes%d" % lo, align_bytes=64))
-            for a in range(lo, hi):
-                r8_codes.append(r8_tiles[-1][:, a - lo, :])
-        for lo, hi in W4_LOADS:
-            w4_tiles.append(keep.tile([P, hi - lo, 2 * N], U8, name="w4_codes%d" % lo, align_bytes=64))
-            for a in range(lo, hi):
-                w4_codes.append(w4_tiles[-1][:, a - lo, :])
-        x_raw = []
-        for a in range(PASSES):
-            x_raw.append(rows_pool.tile([P, PACK, T], F32, name="x_raw%d" % a, align_bytes=256))
+        r8_codes = [keep.tile([P, 4 * N], U8, name="r8_codes%d" % a, align_bytes=64) for a in range(PASSES)]
+        w4_codes = [keep.tile([P, 2 * N], U8, name="w4_codes%d" % a, align_bytes=64) for a in range(PASSES)]
+        x_raw = [rows_pool.tile([P, PACK, T], F32, name="x_raw%d" % a, align_bytes=256) for a in range(PASSES)]
         grouped = {}
         codes = {}
         scales = {}
@@ -63,35 +50,26 @@ def tile_mix_resid_fm_mul_kernel(tc, x, w4_words, w4_scales, r8_words, r8_scales
                 grouped[a, h] = keep.tile([P, T_TILE, PACK], BF16, name="grouped%d%d" % (a, h), align_bytes=64)
                 codes[a, h] = keep.tile([P, T_TILE], U32, name="codes%d%d" % (a, h), align_bytes=64)
                 scales[a, h] = keep.tile([P, T_TILE], U8, name="scales%d%d" % (a, h), align_bytes=64)
-        g_sb = []
-        o_sb = []
-        acc = {}
         drained = rows_pool.tile([P, T_TILE], F32, name="drained", align_bytes=256)
+        g_sb = [rows_pool.tile([P, T], F32, name="g%d" % m, align_bytes=256) for m in range(M_TILES)]
+        o_sb = [rows_pool.tile([P, T], F32, name="o%d" % m, align_bytes=256) for m in range(M_TILES)]
+        acc = {}
         for m in range(M_TILES):
-            g_sb.append(rows_pool.tile([P, T], F32, name="g%d" % m, align_bytes=256))
-        for m in range(M_TILES):
-            o_sb.append(rows_pool.tile([P, T], F32, name="o%d" % m, align_bytes=256))
             for h in range(HALVES):
                 acc[m, h] = psum.tile([P, T_TILE], F32, name="acc%d%d" % (m, h))
 
-        def load_x(a):
-            rows = x[a * K_PASS : (a + 1) * K_PASS, :]
-            nc.sync.dma_start(out=x_raw[a][:], in_=rows.rearrange("(p j) t -> p j t", j=PACK))
+        def load_x(a, first=0, end=PACK):
+            rows = x[a * K_PASS : (a + 1) * K_PASS, :].rearrange("(p j) t -> p j t", j=PACK)
+            nc.sync.dma_start(out=x_raw[a][:, first:end, :], in_=rows[:, first:end, :])
 
-        def load_r8(i):
-            lo, hi = R8_LOADS[i]
+        def load_weights(a):
             nc.sync.dma_start(
-                out=r8_tiles[i][:].bitcast(I32), in_=r8_words[lo:hi].rearrange("a p n i -> p a (n i)").bitcast(I32)
+                out=r8_codes[a][:].bitcast(I32), in_=r8_words[a].rearrange("p n i -> p (n i)").bitcast(I32)
             )
+            nc.sync.dma_start(out=w4_codes[a][:].bitcast(I32), in_=w4_words[a].bitcast(I32))
 
-        def load_w4(i):
-            lo, hi = W4_LOADS[i]
-            nc.sync.dma_start(
-                out=w4_tiles[i][:].bitcast(I32), in_=w4_words[lo:hi].rearrange("a p n -> p a n").bitcast(I32)
-            )
-
-        def load_r8_scales(quads):
-            for q in quads:
+        def load_r8_scales():
+            for q in range(QUADS):
                 nc.sync.dma_start(
                     out=r8_plane[:].bitcast(I32)[32 * q : 32 * q + 16, :],
                     in_=r8_scales[:, 4 * q : 4 * q + 4, :].bitcast(I32),
@@ -104,11 +82,11 @@ def tile_mix_resid_fm_mul_kernel(tc, x, w4_words, w4_scales, r8_words, r8_scales
                     in_=w4_scales[:, r:16:4, :].rearrange("a q n -> q a n").bitcast(I32),
                 )
 
-        def interleave(copy, a, lo, hi):
+        def interleave(copy, a, lo, hi, first=0, end=PACK):
             h, col = divmod(lo, T_TILE)
             copy(
-                out=grouped[a, h][:, col : col + hi - lo, :].rearrange("p (c i) j -> p c j i", i=4),
-                in_=x_raw[a][:, :, lo:hi].rearrange("p j (c i) -> p c j i", i=4),
+                out=grouped[a, h][:, col : col + hi - lo, first:end].rearrange("p (c i) j -> p c j i", i=4),
+                in_=x_raw[a][:, first:end, lo:hi].rearrange("p j (c i) -> p c j i", i=4),
             )
 
         def quantize(a, lo, hi):
@@ -119,13 +97,12 @@ def tile_mix_resid_fm_mul_kernel(tc, x, w4_words, w4_scales, r8_words, r8_scales
                 in_=grouped[a, h][:, col : col + hi - lo, :].rearrange("p c j -> p (c j)"),
             )
 
-        def prepare(a, first, end):
-            v_cols = V_COLS_LAST if (a, first) == (LAST, T_TILE) else V_COLS
-            chunks = range(first, end, CHUNK)
+        def prepare(a, h, v_cols=V_COLS, first=0):
+            chunks = range(h * T_TILE, (h + 1) * T_TILE, CHUNK)
             for lo in chunks:
-                interleave(nc.scalar.copy, a, lo + v_cols, lo + CHUNK)
+                interleave(nc.scalar.copy, a, lo + v_cols, lo + CHUNK, first)
             for lo in chunks:
-                interleave(nc.vector.tensor_copy, a, lo, lo + v_cols)
+                interleave(nc.vector.tensor_copy, a, lo, lo + v_cols, first)
             for lo in chunks:
                 quantize(a, lo, lo + CHUNK)
 
@@ -151,39 +128,55 @@ def tile_mix_resid_fm_mul_kernel(tc, x, w4_words, w4_scales, r8_words, r8_scales
                 stop=(a == LAST and hi == T_TILE),
             )
 
-        steps = [[(multiply, 0, h, 0, T_TILE) for multiply in (multiply_r8, multiply_w4) for h in range(HALVES)]]
-        for a in range(1, LAST):
-            steps.append([(multiply, a, h, 0, T_TILE) for h in range(HALVES) for multiply in (multiply_r8, multiply_w4)])
+        def gate(m, h):
+            cols = slice(h * T_TILE, (h + 1) * T_TILE)
+            nc.vector.tensor_tensor(out=o_sb[m][:, cols], in0=acc[m, h][:], in1=g_sb[m][:, cols], op=MULT)
+
+        def store(m, first, end):
+            cols = slice(first * T_TILE, end * T_TILE)
+            nc.sync.dma_start(out=out[m * P : (m + 1) * P, cols], in_=o_sb[m][:, cols])
 
         with tc.manual_schedule():
             nc.vector.memset(r8_plane[:].bitcast(I32), 0)
             nc.vector.memset(w4_plane[:].rearrange("p a n -> p (a n)").bitcast(I32), 0)
 
             load_x(0)
-            load_r8_scales(range(QUADS))
-            load_r8(0)
-            load_w4(0)
-            load_x(1)
+            load_r8_scales()
+            load_weights(0)
+            load_x(1, 0, 2)
             load_w4_scales()
-            load_r8(1)
-            load_w4(1)
-            for a in range(2, PASSES):
-                load_x(a)
-                load_r8(a)
-                load_w4(a)
+            load_x(1, 2, PACK)
+            load_weights(1)
+            load_x(2)
+            load_weights(2)
+            load_x(LAST, 0, 2)
+            load_x(LAST, 2, PACK)
+            load_weights(LAST)
             for m in range(M_TILES):
                 nc.sync.dma_start(out=g_sb[m][:], in_=g[m * P : (m + 1) * P, :])
 
-            for a in range(LAST):
-                width = T if a == 0 else T_TILE
-                for first in range(0, T, width):
-                    prepare(a, first, first + width)
-                for multiply, b, h, lo, hi in steps[a]:
+            for h in range(HALVES):
+                prepare(0, h)
+            for multiply in (multiply_r8, multiply_w4):
+                for h in range(HALVES):
                     for m in range(M_TILES):
-                        multiply(b, m, h, lo, hi)
+                        multiply(0, m, h)
 
-            for first in range(0, T, T_TILE):
-                prepare(LAST, first, first + T_TILE)
+            for a in range(1, LAST):
+                for h in range(HALVES):
+                    prepare(a, h)
+                for lo in range(0, T_TILE, CHUNK):
+                    for m in range(M_TILES):
+                        multiply_r8(a, m, 0, lo, lo + CHUNK)
+                for multiply, h in ((multiply_w4, 0), (multiply_r8, 1), (multiply_w4, 1)):
+                    for m in range(M_TILES):
+                        multiply(a, m, h)
+
+            for lo in range(0, T, T_TILE):
+                interleave(nc.scalar.copy, LAST, lo + V_COLS_EARLY, lo + T_TILE, 0, 2)
+                interleave(nc.vector.tensor_copy, LAST, lo, lo + V_COLS_EARLY, 0, 2)
+            for h in range(HALVES):
+                prepare(LAST, h, V_COLS_LATE[h], 2)
             for lo in range(0, T_TILE, CHUNK):
                 for m in range(2):
                     multiply_r8(LAST, m, 0, lo, lo + CHUNK)
@@ -192,14 +185,13 @@ def tile_mix_resid_fm_mul_kernel(tc, x, w4_words, w4_scales, r8_words, r8_scales
                 multiply_r8(LAST, m, h)
                 multiply_w4(LAST, m, h)
             nc.scalar.copy(out=drained[:], in_=acc[2, 0][:])
-            nc.gpsimd.tensor_tensor(
-                out=o_sb[2][:, :T_TILE], in0=drained[:], in1=g_sb[2][:, :T_TILE], op=mybir.AluOpType.mult
-            )
-            for m, h in ((0, 0), (1, 0), (0, 1), (1, 1), (2, 1), (3, 0), (3, 1)):
-                cols = slice(h * T_TILE, (h + 1) * T_TILE)
-                nc.vector.tensor_tensor(
-                    out=o_sb[m][:, cols], in0=acc[m, h][:], in1=g_sb[m][:, cols], op=mybir.AluOpType.mult
-                )
-                nc.sync.dma_start(out=out[m * P : (m + 1) * P, cols], in_=o_sb[m][:, cols])
-                if (m, h) == (2, 1):
-                    nc.sync.dma_start(out=out[m * P : (m + 1) * P, :T_TILE], in_=o_sb[m][:, :T_TILE])
+            nc.gpsimd.tensor_tensor(out=o_sb[2][:, :T_TILE], in0=drained[:], in1=g_sb[2][:, :T_TILE], op=MULT)
+            for h in range(HALVES):
+                for m in range(2):
+                    gate(m, h)
+                    store(m, h, h + 1)
+            gate(2, 1)
+            store(2, 0, HALVES)
+            for h in range(HALVES):
+                gate(3, h)
+            store(3, 0, HALVES)

@@ -26,7 +26,7 @@ HALVES = T // T_TILE
 QUADS = 4
 CHUNK = 256
 V_COLS = 168
-V_COLS_LATE = (144, 96)
+LATE_CHUNKS = ((0, 256, 144), (256, 512, 144), (512, 768, 136), (768, 896, 0), (896, 1024, 0))
 V_COLS_EARLY = 336
 
 
@@ -50,7 +50,6 @@ def tile_mix_resid_fm_mul_kernel(tc, x, w4_words, w4_scales, r8_words, r8_scales
                 grouped[a, h] = keep.tile([P, T_TILE, PACK], BF16, name="grouped%d%d" % (a, h), align_bytes=64)
                 codes[a, h] = keep.tile([P, T_TILE], U32, name="codes%d%d" % (a, h), align_bytes=64)
                 scales[a, h] = keep.tile([P, T_TILE], U8, name="scales%d%d" % (a, h), align_bytes=64)
-        drained = rows_pool.tile([P, T_TILE], F32, name="drained", align_bytes=256)
         g_sb = [rows_pool.tile([P, T], F32, name="g%d" % m, align_bytes=256) for m in range(M_TILES)]
         o_sb = [rows_pool.tile([P, T], F32, name="o%d" % m, align_bytes=256) for m in range(M_TILES)]
         acc = {}
@@ -128,14 +127,6 @@ def tile_mix_resid_fm_mul_kernel(tc, x, w4_words, w4_scales, r8_words, r8_scales
                 stop=(a == LAST and hi == T_TILE),
             )
 
-        def gate(m, h):
-            cols = slice(h * T_TILE, (h + 1) * T_TILE)
-            nc.vector.tensor_tensor(out=o_sb[m][:, cols], in0=acc[m, h][:], in1=g_sb[m][:, cols], op=MULT)
-
-        def store(m, first, end):
-            cols = slice(first * T_TILE, end * T_TILE)
-            nc.sync.dma_start(out=out[m * P : (m + 1) * P, cols], in_=o_sb[m][:, cols])
-
         with tc.manual_schedule():
             nc.vector.memset(r8_plane[:].bitcast(I32), 0)
             nc.vector.memset(w4_plane[:].rearrange("p a n -> p (a n)").bitcast(I32), 0)
@@ -175,23 +166,26 @@ def tile_mix_resid_fm_mul_kernel(tc, x, w4_words, w4_scales, r8_words, r8_scales
             for lo in range(0, T, T_TILE):
                 interleave(nc.scalar.copy, LAST, lo + V_COLS_EARLY, lo + T_TILE, 0, 2)
                 interleave(nc.vector.tensor_copy, LAST, lo, lo + V_COLS_EARLY, 0, 2)
-            for h in range(HALVES):
-                prepare(LAST, h, V_COLS_LATE[h], 2)
-            for lo in range(0, T_TILE, CHUNK):
-                for m in range(2):
-                    multiply_r8(LAST, m, 0, lo, lo + CHUNK)
-                    multiply_w4(LAST, m, 0, lo, lo + CHUNK)
-            for m, h in ((2, 0), (0, 1), (1, 1), (2, 1), (3, 0), (3, 1)):
+            for lo, hi, v_cols in LATE_CHUNKS:
+                interleave(nc.scalar.copy, LAST, lo + v_cols, hi, 2)
+            for i, (lo, hi, v_cols) in enumerate(LATE_CHUNKS):
+                if v_cols:
+                    interleave(nc.vector.tensor_copy, LAST, lo, lo + v_cols, 2)
+                if i:
+                    quantize(LAST, *LATE_CHUNKS[i - 1][:2])
+            quantize(LAST, *LATE_CHUNKS[-1][:2])
+            for lo, hi, v_cols in LATE_CHUNKS:
+                h, col = divmod(lo, T_TILE)
+                multiply_r8(LAST, 0, h, col, col + hi - lo)
+                multiply_w4(LAST, 0, h, col, col + hi - lo)
+                if lo < T_TILE:
+                    multiply_r8(LAST, 1, 0, lo, hi)
+            multiply_w4(LAST, 1, 0)
+            for m, h in ((1, 1), (2, 0), (2, 1), (3, 0), (3, 1)):
                 multiply_r8(LAST, m, h)
                 multiply_w4(LAST, m, h)
-            nc.scalar.copy(out=drained[:], in_=acc[2, 0][:])
-            nc.gpsimd.tensor_tensor(out=o_sb[2][:, :T_TILE], in0=drained[:], in1=g_sb[2][:, :T_TILE], op=MULT)
-            for h in range(HALVES):
-                for m in range(2):
-                    gate(m, h)
-                    store(m, h, h + 1)
-            gate(2, 1)
-            store(2, 0, HALVES)
-            for h in range(HALVES):
-                gate(3, h)
-            store(3, 0, HALVES)
+            for m in range(M_TILES):
+                for h in range(HALVES):
+                    cols = slice(h * T_TILE, (h + 1) * T_TILE)
+                    nc.vector.tensor_tensor(out=o_sb[m][:, cols], in0=acc[m, h][:], in1=g_sb[m][:, cols], op=MULT)
+                nc.sync.dma_start(out=out[m * P : (m + 1) * P, :], in_=o_sb[m][:])

@@ -61,10 +61,12 @@ def tile_mix_resid_fm_mul_kernel(tc, x, w4_words, w4_scales, r8_words, r8_scales
             rows = x[a * K_PASS : (a + 1) * K_PASS, :].rearrange("(p j) t -> p j t", j=PACK)
             nc.sync.dma_start(out=x_raw[a][:, first:end, :], in_=rows[:, first:end, :])
 
-        def load_weights(a):
+        def load_r8(a):
             nc.sync.dma_start(
                 out=r8_codes[a][:].bitcast(I32), in_=r8_words[a].rearrange("p n i -> p (n i)").bitcast(I32)
             )
+
+        def load_w4(a):
             nc.sync.dma_start(out=w4_codes[a][:].bitcast(I32), in_=w4_words[a].bitcast(I32))
 
         def load_r8_scales():
@@ -74,12 +76,11 @@ def tile_mix_resid_fm_mul_kernel(tc, x, w4_words, w4_scales, r8_words, r8_scales
                     in_=r8_scales[:, 4 * q : 4 * q + 4, :].bitcast(I32),
                 )
 
-        def load_w4_scales():
-            for r in range(4):
-                nc.sync.dma_start(
-                    out=w4_plane[r:P:32, :, :].bitcast(I32),
-                    in_=w4_scales[:, r:16:4, :].rearrange("a q n -> q a n").bitcast(I32),
-                )
+        def load_w4_scales(r, first, end):
+            nc.sync.dma_start(
+                out=w4_plane[r:P:32, first:end, :].bitcast(I32),
+                in_=w4_scales[first:end, r:16:4, :].rearrange("a q n -> q a n").bitcast(I32),
+            )
 
         def interleave(copy, a, lo, hi, first=0, end=PACK):
             h, col = divmod(lo, T_TILE)
@@ -96,12 +97,12 @@ def tile_mix_resid_fm_mul_kernel(tc, x, w4_words, w4_scales, r8_words, r8_scales
                 in_=grouped[a, h][:, col : col + hi - lo, :].rearrange("p c j -> p (c j)"),
             )
 
-        def prepare(a, h, v_cols=V_COLS, first=0):
-            chunks = range(h * T_TILE, (h + 1) * T_TILE, CHUNK)
+        def prepare(a, first, end):
+            chunks = range(first, end, CHUNK)
             for lo in chunks:
-                interleave(nc.scalar.copy, a, lo + v_cols, lo + CHUNK, first)
+                interleave(nc.scalar.copy, a, lo + V_COLS, lo + CHUNK)
             for lo in chunks:
-                interleave(nc.vector.tensor_copy, a, lo, lo + v_cols, first)
+                interleave(nc.vector.tensor_copy, a, lo, lo + V_COLS)
             for lo in chunks:
                 quantize(a, lo, lo + CHUNK)
 
@@ -133,29 +134,36 @@ def tile_mix_resid_fm_mul_kernel(tc, x, w4_words, w4_scales, r8_words, r8_scales
 
             load_x(0)
             load_r8_scales()
-            load_weights(0)
-            load_x(1, 0, 2)
-            load_w4_scales()
-            load_x(1, 2, PACK)
-            load_weights(1)
+            load_r8(0)
+            load_w4(0)
+            load_x(1)
+            for r in range(4):
+                load_w4_scales(r, 0, 2)
+            load_r8(1)
+            load_w4(1)
             load_x(2)
-            load_weights(2)
+            load_r8(2)
+            for r in range(4):
+                load_w4_scales(r, 2, LAST if r else PASSES)
+            load_w4(2)
             load_x(LAST, 0, 2)
             load_x(LAST, 2, PACK)
-            load_weights(LAST)
+            load_r8(LAST)
+            for r in range(1, 4):
+                load_w4_scales(r, LAST, PASSES)
+            load_w4(LAST)
             for m in range(M_TILES):
                 nc.sync.dma_start(out=g_sb[m][:], in_=g[m * P : (m + 1) * P, :])
 
-            for h in range(HALVES):
-                prepare(0, h)
+            prepare(0, 0, T)
             for multiply in (multiply_r8, multiply_w4):
                 for h in range(HALVES):
                     for m in range(M_TILES):
                         multiply(0, m, h)
 
             for a in range(1, LAST):
-                for h in range(HALVES):
-                    prepare(a, h)
+                for first in range(0, T, T_TILE):
+                    prepare(a, first, first + T_TILE)
                 for lo in range(0, T_TILE, CHUNK):
                     for m in range(M_TILES):
                         multiply_r8(a, m, 0, lo, lo + CHUNK)
@@ -188,4 +196,7 @@ def tile_mix_resid_fm_mul_kernel(tc, x, w4_words, w4_scales, r8_words, r8_scales
                 for h in range(HALVES):
                     cols = slice(h * T_TILE, (h + 1) * T_TILE)
                     nc.vector.tensor_tensor(out=o_sb[m][:, cols], in0=acc[m, h][:], in1=g_sb[m][:, cols], op=MULT)
-                nc.sync.dma_start(out=out[m * P : (m + 1) * P, :], in_=o_sb[m][:])
+                    if m == 0:
+                        nc.sync.dma_start(out=out[:P, cols], in_=o_sb[0][:, cols])
+                if m:
+                    nc.sync.dma_start(out=out[m * P : (m + 1) * P, :], in_=o_sb[m][:])

@@ -37,7 +37,8 @@ def tile_mix_resid_fm_mul_kernel(tc, x, w4_words, w4_scales, r8_words, r8_scales
         rows_pool = ctx.enter_context(tc.tile_pool(name="rows", bufs=1))
         psum = ctx.enter_context(tc.psum_pool(name="psum", bufs=1))
 
-        r8_plane = keep.tile([P, N], U8, name="r8_plane", align_bytes=64)
+        r8_rows = keep.tile([P, 2, N], U8, name="r8_rows", align_bytes=64)
+        r8_plane = r8_rows[:, 0, :]
         w4_plane = keep.tile([P, PASSES, N], U8, name="w4_plane", align_bytes=64)
         r8_codes = [keep.tile([P, 4 * N], U8, name="r8_codes%d" % a, align_bytes=64) for a in range(PASSES)]
         w4_codes = [keep.tile([P, 2 * N], U8, name="w4_codes%d" % a, align_bytes=64) for a in range(PASSES)]
@@ -72,7 +73,7 @@ def tile_mix_resid_fm_mul_kernel(tc, x, w4_words, w4_scales, r8_words, r8_scales
         def load_r8_scales():
             for q in range(QUADS):
                 nc.sync.dma_start(
-                    out=r8_plane[:].bitcast(I32)[32 * q : 32 * q + 16, :],
+                    out=r8_rows[32 * (q % 2) : 32 * (q % 2) + 16, q // 2, :].bitcast(I32),
                     in_=r8_scales[:, 4 * q : 4 * q + 4, :].bitcast(I32),
                 )
 
@@ -97,13 +98,13 @@ def tile_mix_resid_fm_mul_kernel(tc, x, w4_words, w4_scales, r8_words, r8_scales
                 in_=grouped[a, h][:, col : col + hi - lo, :].rearrange("p c j -> p (c j)"),
             )
 
-        def prepare(a, first, end):
-            chunks = range(first, end, CHUNK)
-            for lo in chunks:
+        def interleave_chunks(a, first, end):
+            for lo in range(first, end, CHUNK):
                 interleave(nc.scalar.copy, a, lo + V_COLS, lo + CHUNK)
-            for lo in chunks:
                 interleave(nc.vector.tensor_copy, a, lo, lo + V_COLS)
-            for lo in chunks:
+
+        def quantize_chunks(a, first, end):
+            for lo in range(first, end, CHUNK):
                 quantize(a, lo, lo + CHUNK)
 
         def multiply_r8(a, m, h, lo=0, hi=T_TILE):
@@ -129,7 +130,7 @@ def tile_mix_resid_fm_mul_kernel(tc, x, w4_words, w4_scales, r8_words, r8_scales
             )
 
         with tc.manual_schedule():
-            nc.vector.memset(r8_plane[:].bitcast(I32), 0)
+            nc.vector.memset(r8_rows[: P // 2].rearrange("p u n -> p (u n)").bitcast(I32), 0)
             nc.vector.memset(w4_plane[:].rearrange("p a n -> p (a n)").bitcast(I32), 0)
 
             load_x(0)
@@ -155,7 +156,9 @@ def tile_mix_resid_fm_mul_kernel(tc, x, w4_words, w4_scales, r8_words, r8_scales
             for m in range(M_TILES):
                 nc.sync.dma_start(out=g_sb[m][:], in_=g[m * P : (m + 1) * P, :])
 
-            prepare(0, 0, T)
+            interleave_chunks(0, 0, T)
+            nc.vector.tensor_copy(out=r8_rows[P // 2 :, 0, :].bitcast(I32), in_=r8_rows[: P // 2, 1, :].bitcast(I32))
+            quantize_chunks(0, 0, T)
             for multiply in (multiply_r8, multiply_w4):
                 for h in range(HALVES):
                     for m in range(M_TILES):
@@ -163,7 +166,8 @@ def tile_mix_resid_fm_mul_kernel(tc, x, w4_words, w4_scales, r8_words, r8_scales
 
             for a in range(1, LAST):
                 for first in range(0, T, T_TILE):
-                    prepare(a, first, first + T_TILE)
+                    interleave_chunks(a, first, first + T_TILE)
+                    quantize_chunks(a, first, first + T_TILE)
                 for lo in range(0, T_TILE, CHUNK):
                     for m in range(M_TILES):
                         multiply_r8(a, m, 0, lo, lo + CHUNK)

@@ -39,7 +39,7 @@ def tile_mix_resid_fm_mul_kernel(tc, x, w4_words, w4_scales, r8_words, r8_scales
 
         r8_rows = keep.tile([P, 2, N], U8, name="r8_rows", align_bytes=64)
         r8_plane = r8_rows[:, 0, :]
-        w4_plane = keep.tile([P, PASSES, N], U8, name="w4_plane", align_bytes=64)
+        w4_plane = keep.tile([P, PASSES + 1, N], U8, name="w4_plane", align_bytes=64)
         r8_codes = [keep.tile([P, 4 * N], U8, name="r8_codes%d" % a, align_bytes=64) for a in range(PASSES)]
         w4_codes = [keep.tile([P, 2 * N], U8, name="w4_codes%d" % a, align_bytes=64) for a in range(PASSES)]
         x_raw = [rows_pool.tile([P, PACK, T], F32, name="x_raw%d" % a, align_bytes=256) for a in range(PASSES)]
@@ -131,7 +131,7 @@ def tile_mix_resid_fm_mul_kernel(tc, x, w4_words, w4_scales, r8_words, r8_scales
 
         with tc.manual_schedule():
             nc.vector.memset(r8_rows[: P // 2].rearrange("p u n -> p (u n)").bitcast(I32), 0)
-            nc.vector.memset(w4_plane[:].rearrange("p a n -> p (a n)").bitcast(I32), 0)
+            nc.vector.memset(w4_plane[:, :PASSES, :].rearrange("p a n -> p (a n)").bitcast(I32), 0)
 
             load_x(0)
             load_r8_scales()
@@ -145,9 +145,13 @@ def tile_mix_resid_fm_mul_kernel(tc, x, w4_words, w4_scales, r8_words, r8_scales
             load_x(2)
             load_r8(2)
             for r in range(4):
-                load_w4_scales(r, 2, LAST if r else PASSES)
+                nc.sync.dma_start(
+                    out=w4_plane[r:P:64, 2 : PASSES + 1 : 2, :].bitcast(I32),
+                    in_=w4_scales[2, r:16:4, :].rearrange("(u v) n -> u v n", v=2).bitcast(I32),
+                )
             load_w4(2)
             load_x(LAST, 0, 2)
+            load_w4_scales(0, LAST, PASSES)
             load_x(LAST, 2, PACK)
             load_r8(LAST)
             for r in range(1, 4):
@@ -168,6 +172,12 @@ def tile_mix_resid_fm_mul_kernel(tc, x, w4_words, w4_scales, r8_words, r8_scales
                 for first in range(0, T, T_TILE):
                     interleave_chunks(a, first, first + T_TILE)
                     quantize_chunks(a, first, first + T_TILE)
+                    if (a, first) == (2, 0):
+                        for low in (0, 64):
+                            nc.vector.tensor_copy(
+                                out=w4_plane[low + 32 : low + 36, 2, :].bitcast(I32),
+                                in_=w4_plane[low : low + 4, PASSES, :].bitcast(I32),
+                            )
                 for lo in range(0, T_TILE, CHUNK):
                     for m in range(M_TILES):
                         multiply_r8(a, m, 0, lo, lo + CHUNK)

@@ -37,11 +37,11 @@ def tile_mix_resid_fm_mul_kernel(tc, x, w4_words, w4_scales, r8_words, r8_scales
         rows_pool = ctx.enter_context(tc.tile_pool(name="rows", bufs=1))
         psum = ctx.enter_context(tc.psum_pool(name="psum", bufs=1))
 
-        r8_rows = keep.tile([P, 2, N], U8, name="r8_rows", align_bytes=64)
+        r8_rows = rows_pool.tile([P, 2, N], U8, name="r8_rows", align_bytes=256)
         r8_plane = r8_rows[:, 0, :]
-        w4_plane = keep.tile([P, PASSES + 1, N], U8, name="w4_plane", align_bytes=64)
-        r8_codes = [keep.tile([P, 4 * N], U8, name="r8_codes%d" % a, align_bytes=64) for a in range(PASSES)]
-        w4_codes = [keep.tile([P, 2 * N], U8, name="w4_codes%d" % a, align_bytes=64) for a in range(PASSES)]
+        w4_plane = rows_pool.tile([P, PASSES + 1, N], U8, name="w4_plane", align_bytes=256)
+        r8_codes = [rows_pool.tile([P, 4 * N], U8, name="r8_codes%d" % a, align_bytes=256) for a in range(PASSES)]
+        w4_codes = [rows_pool.tile([P, 2 * N], U8, name="w4_codes%d" % a, align_bytes=256) for a in range(PASSES)]
         x_raw = [rows_pool.tile([P, PACK, T], F32, name="x_raw%d" % a, align_bytes=256) for a in range(PASSES)]
         grouped = {}
         codes = {}

from contextlib import ExitStack

import concourse.mybir as mybir

K, N, T = 2048, 512, 1024

F32 = mybir.dt.float32
BF16 = mybir.dt.bfloat16
I32 = mybir.dt.int32
U32 = mybir.dt.uint32
U8 = mybir.dt.uint8
FP8X4 = mybir.dt.float8_e4m3fn_x4
FP4X4 = mybir.dt.float4_e2m1fn_x4
MULT = mybir.AluOpType.mult

FLOPS = 2 * 2 * K * N * T

P = 128
PACK = 4
K_PASS = P * PACK
PASSES = K // K_PASS
LAST = PASSES - 1
M_TILES = N // P
T_TILE = 512
HALVES = T // T_TILE
QUADS = 4
CHUNK = 256
V_COLS = 168
LATE_CHUNKS = ((0, 256, 144), (256, 512, 144), (512, 768, 136), (768, 896, 0), (896, 1024, 0))
V_COLS_EARLY = 336


def tile_mix_resid_fm_mul_kernel(tc, x, w4_words, w4_scales, r8_words, r8_scales, g, out):
    nc = tc.nc
    with ExitStack() as ctx:
        keep = ctx.enter_context(tc.tile_pool(name="keep", bufs=1))
        rows_pool = ctx.enter_context(tc.tile_pool(name="rows", bufs=1))
        psum = ctx.enter_context(tc.psum_pool(name="psum", bufs=1))

        r8_rows = rows_pool.tile([P, 2, N], U8, name="r8_rows", align_bytes=256)
        r8_plane = r8_rows[:, 0, :]
        w4_plane = rows_pool.tile([P, PASSES + 1, N], U8, name="w4_plane", align_bytes=256)
        r8_codes = [rows_pool.tile([P, 4 * N], U8, name="r8_codes%d" % a, align_bytes=256) for a in range(PASSES)]
        w4_codes = [rows_pool.tile([P, 2 * N], U8, name="w4_codes%d" % a, align_bytes=256) for a in range(PASSES)]
        x_raw = [rows_pool.tile([P, PACK, T], F32, name="x_raw%d" % a, align_bytes=256) for a in range(PASSES)]
        grouped = {}
        codes = {}
        scales = {}
        for a in range(PASSES):
            for h in range(HALVES):
                grouped[a, h] = keep.tile([P, T_TILE, PACK], BF16, name="grouped%d%d" % (a, h), align_bytes=64)
                codes[a, h] = keep.tile([P, T_TILE], U32, name="codes%d%d" % (a, h), align_bytes=64)
                scales[a, h] = keep.tile([P, T_TILE], U8, name="scales%d%d" % (a, h), align_bytes=64)
        g_sb = [rows_pool.tile([P, T], F32, name="g%d" % m, align_bytes=256) for m in range(M_TILES)]
        o_sb = [rows_pool.tile([P, T], F32, name="o%d" % m, align_bytes=256) for m in range(M_TILES)]
        acc = {}
        for m in range(M_TILES):
            for h in range(HALVES):
                acc[m, h] = psum.tile([P, T_TILE], F32, name="acc%d%d" % (m, h))

        def load_x(a, first=0, end=PACK):
            rows = x[a * K_PASS : (a + 1) * K_PASS, :].rearrange("(p j) t -> p j t", j=PACK)
            nc.sync.dma_start(out=x_raw[a][:, first:end, :], in_=rows[:, first:end, :])

        def load_r8(a):
            nc.sync.dma_start(
                out=r8_codes[a][:].bitcast(I32), in_=r8_words[a].rearrange("p n i -> p (n i)").bitcast(I32)
            )

        def load_w4(a):
            nc.sync.dma_start(out=w4_codes[a][:].bitcast(I32), in_=w4_words[a].bitcast(I32))

        def load_r8_scales():
            for q in range(QUADS):
                nc.sync.dma_start(
                    out=r8_rows[32 * (q % 2) : 32 * (q % 2) + 16, q // 2, :].bitcast(I32),
                    in_=r8_scales[:, 4 * q : 4 * q + 4, :].bitcast(I32),
                )

        def load_w4_scales(r, first, end):
            nc.sync.dma_start(
                out=w4_plane[r:P:32, first:end, :].bitcast(I32),
                in_=w4_scales[first:end, r:16:4, :].rearrange("a q n -> q a n").bitcast(I32),
            )

        def interleave(copy, a, lo, hi, first=0, end=PACK):
            h, col = divmod(lo, T_TILE)
            copy(
                out=grouped[a, h][:, col : col + hi - lo, first:end].rearrange("p (c i) j -> p c j i", i=4),
                in_=x_raw[a][:, first:end, lo:hi].rearrange("p j (c i) -> p c j i", i=4),
            )

        def quantize(a, lo, hi):
            h, col = divmod(lo, T_TILE)
            nc.vector.quantize_mx(
                out=codes[a, h][:, col : col + hi - lo].bitcast(FP8X4),
                scales=scales[a, h][:, col : col + hi - lo],
                in_=grouped[a, h][:, col : col + hi - lo, :].rearrange("p c j -> p (c j)"),
            )

        def interleave_chunks(a, first, end):
            for lo in range(first, end, CHUNK):
                interleave(nc.scalar.copy, a, lo + V_COLS, lo + CHUNK)
                interleave(nc.vector.tensor_copy, a, lo, lo + V_COLS)

        def quantize_chunks(a, first, end):
            for lo in range(first, end, CHUNK):
                quantize(a, lo, lo + CHUNK)

        def multiply_r8(a, m, h, lo=0, hi=T_TILE):
            nc.tensor.matmul_mx(
                out=acc[m, h][:, lo:hi],
                lhsT=r8_codes[a][:, 4 * P * m : 4 * P * (m + 1)].bitcast(FP8X4),
                lhsT_scale=r8_plane[4 * a : P, P * m : P * (m + 1)],
                rhs=codes[a, h][:, lo:hi].bitcast(FP8X4),
                rhs_scale=scales[a, h][:, lo:hi],
                start=(a == 0 and lo == 0),
                stop=False,
            )

        def multiply_w4(a, m, h, lo=0, hi=T_TILE):
            nc.tensor.matmul_mx(
                out=acc[m, h][:, lo:hi],
                lhsT=w4_codes[a][:, 2 * P * m : 2 * P * (m + 1)].bitcast(FP4X4),
                lhsT_scale=w4_plane[:, a, P * m : P * (m + 1)],
                rhs=codes[a, h][:, lo:hi].bitcast(FP8X4),
                rhs_scale=scales[a, h][:, lo:hi],
                start=False,
                stop=(a == LAST and hi == T_TILE),
            )

        with tc.manual_schedule():
            nc.vector.memset(r8_rows[: P // 2].rearrange("p u n -> p (u n)").bitcast(I32), 0)
            nc.vector.memset(w4_plane[:, :PASSES, :].rearrange("p a n -> p (a n)").bitcast(I32), 0)

            load_x(0)
            load_r8_scales()
            load_r8(0)
            load_w4(0)
            load_x(1)
            for r in range(4):
                load_w4_scales(r, 0, 2)
            load_r8(1)
            load_w4(1)
            load_x(2)
            load_r8(2)
            for r in range(4):
                nc.sync.dma_start(
                    out=w4_plane[r:P:64, 2 : PASSES + 1 : 2, :].bitcast(I32),
                    in_=w4_scales[2, r:16:4, :].rearrange("(u v) n -> u v n", v=2).bitcast(I32),
                )
            load_w4(2)
            load_x(LAST, 0, 2)
            load_w4_scales(0, LAST, PASSES)
            load_x(LAST, 2, PACK)
            load_r8(LAST)
            for r in range(1, 4):
                load_w4_scales(r, LAST, PASSES)
            load_w4(LAST)
            for m in range(M_TILES):
                nc.sync.dma_start(out=g_sb[m][:], in_=g[m * P : (m + 1) * P, :])

            interleave_chunks(0, 0, T)
            nc.vector.tensor_copy(out=r8_rows[P // 2 :, 0, :].bitcast(I32), in_=r8_rows[: P // 2, 1, :].bitcast(I32))
            quantize_chunks(0, 0, T)
            for multiply in (multiply_r8, multiply_w4):
                for h in range(HALVES):
                    for m in range(M_TILES):
                        multiply(0, m, h)

            for a in range(1, LAST):
                for first in range(0, T, T_TILE):
                    interleave_chunks(a, first, first + T_TILE)
                    quantize_chunks(a, first, first + T_TILE)
                    if (a, first) == (2, 0):
                        for low in (0, 64):
                            nc.vector.tensor_copy(
                                out=w4_plane[low + 32 : low + 36, 2, :].bitcast(I32),
                                in_=w4_plane[low : low + 4, PASSES, :].bitcast(I32),
                            )
                for lo in range(0, T_TILE, CHUNK):
                    for m in range(M_TILES):
                        multiply_r8(a, m, 0, lo, lo + CHUNK)
                for multiply, h in ((multiply_w4, 0), (multiply_r8, 1), (multiply_w4, 1)):
                    for m in range(M_TILES):
                        multiply(a, m, h)

            for lo in range(0, T, T_TILE):
                interleave(nc.scalar.copy, LAST, lo + V_COLS_EARLY, lo + T_TILE, 0, 2)
                interleave(nc.vector.tensor_copy, LAST, lo, lo + V_COLS_EARLY, 0, 2)
            for lo, hi, v_cols in LATE_CHUNKS:
                interleave(nc.scalar.copy, LAST, lo + v_cols, hi, 2)
            for i, (lo, hi, v_cols) in enumerate(LATE_CHUNKS):
                if v_cols:
                    interleave(nc.vector.tensor_copy, LAST, lo, lo + v_cols, 2)
                if i:
                    quantize(LAST, *LATE_CHUNKS[i - 1][:2])
            quantize(LAST, *LATE_CHUNKS[-1][:2])
            for lo, hi, v_cols in LATE_CHUNKS:
                h, col = divmod(lo, T_TILE)
                multiply_r8(LAST, 0, h, col, col + hi - lo)
                multiply_w4(LAST, 0, h, col, col + hi - lo)
                if lo < T_TILE:
                    multiply_r8(LAST, 1, 0, lo, hi)
            multiply_w4(LAST, 1, 0)
            for m, h in ((1, 1), (2, 0), (2, 1), (3, 0), (3, 1)):
                multiply_r8(LAST, m, h)
                multiply_w4(LAST, m, h)
            for m in range(M_TILES):
                for h in range(HALVES):
                    cols = slice(h * T_TILE, (h + 1) * T_TILE)
                    nc.vector.tensor_tensor(out=o_sb[m][:, cols], in0=acc[m, h][:], in1=g_sb[m][:, cols], op=MULT)
                    if m == 0:
                        nc.sync.dma_start(out=out[:P, cols], in_=o_sb[0][:, cols])
                if m:
                    nc.sync.dma_start(out=out[m * P : (m + 1) * P, :], in_=o_sb[m][:])
